import numpy as np
import ml_dtypes


def mxq(x, axis, fmt="e4m3"):
    dtype, down = {"e4m3": (ml_dtypes.float8_e4m3fn, 7), "e5m2": (ml_dtypes.float8_e5m2, 14)}[fmt]
    v = np.moveaxis(np.asarray(x, np.float32).astype(ml_dtypes.bfloat16).astype(np.float64), axis, -1)
    blocks = v.reshape(v.shape[:-1] + (-1, 32))
    amax = np.abs(blocks).max(-1, keepdims=True)
    byte = np.maximum(np.where(amax > 0, np.frexp(amax)[1] - 1 + 127, 0) - down, 1)
    scale = np.exp2(byte - 127.0)
    codes = (blocks / scale).astype(np.float32).astype(dtype).astype(np.float64)
    return np.moveaxis((codes * scale).reshape(v.shape), -1, axis)


WIDE = False


def mx_kscale(k):
    if not WIDE:
        return np.ones(k)
    levels = np.array([10, -10, 5, -5, 0])
    if k % 512:
        return np.exp2(np.random.permutation(np.resize(levels, k // 32))).repeat(32)
    a = np.empty((k // 512, 16))
    for p in range(k // 512):
        a[p, :8] = np.random.permutation(np.resize(levels, 8))
        for g in range(8):
            far = levels[np.abs(levels - a[p, g]) >= 10]
            a[p, g + 8] = far[np.random.randint(len(far))]
    return np.exp2(a.ravel()).repeat(32)


def f64(x):
    return np.asarray(x).astype(np.float64)


def striped(idx):
    return np.tile(idx.reshape(-1, 16).T, (8, 1)).astype(np.uint16)


def unstriped(offs):
    return offs[:16].T.reshape(-1).astype(np.int64)


def striped8(idx):
    return np.concatenate([x.reshape(-1, 16).T for x in idx]).astype(np.uint16)


def runs(offs, k):
    lists = np.stack([offs[16 * r : 16 * r + 16].T.reshape(-1) for r in range(8)]).astype(np.int64)
    return lists[np.arange(k) % 512 // 64]


def pack_weight(w):
    k, n = w.shape
    w = f64(np.asarray(w, np.float32).astype(ml_dtypes.bfloat16)).reshape(k // 32, 32, n)
    amax = np.abs(w).max(1)
    byte = np.clip(np.where(amax > 0, np.frexp(amax)[1] - 1 + 127 - 7, 1), 1, 254)
    scaled = (w * np.exp2(127.0 - byte)[:, None, :]).reshape(k, n).astype(np.float32)
    words = np.ascontiguousarray(scaled.reshape(k // 512, 128, 4, n).transpose(0, 1, 3, 2)).astype(ml_dtypes.float8_e4m3fn).view(np.uint8)
    return words, np.ascontiguousarray(byte.astype(np.uint8).reshape(k // 512, 16, n))


def unpack_weight(words, scales):
    g, p, n, _ = words.shape
    vals = np.ascontiguousarray(words).view(ml_dtypes.float8_e4m3fn).astype(np.float64) * np.repeat(np.exp2(scales.astype(np.float64) - 127.0), 8, axis=1)[..., None]
    return vals.transpose(0, 1, 3, 2).reshape(g * 512, n)


def relu(v):
    return np.maximum(v, 0.0)


def sigmoid(v):
    return 1.0 / (1.0 + np.exp(-np.maximum(v, -700.0)))

def planes(y):
    n, m = y.shape
    v = y.astype(np.float32).astype(ml_dtypes.bfloat16).astype(np.float64).reshape(n // 32, 32, m)
    top = np.abs(v).max(1)
    byte = np.clip(np.where(top > 0, np.frexp(top)[1] - 1 + 127 - 7, 1), 1, 254)
    codes = (v * np.exp2(127.0 - byte)[:, None, :]).reshape(n, m).astype(np.float32).astype(ml_dtypes.float8_e4m3fn).view(np.uint8)
    words = codes.reshape(n // 512, 128, 4, m).transpose(0, 1, 3, 2)
    return np.ascontiguousarray(words), np.ascontiguousarray(byte.astype(np.uint8).reshape(n // 512, 16, m))


K, T, S, N, H = 512, 2048, 512, 512, 512


def setup_inputs():
    n = np.random.standard_normal
    s = mx_kscale(K)[:, None]
    u = mx_kscale(H)
    packed_xT = pack_weight(n((K, T)) * s)
    packed_w1 = pack_weight(n((K, H)) / np.sqrt(K) / s)
    packed_w2 = pack_weight(n((H, N)) / np.sqrt(H) / u[:, None])
    return {
        "x_words": packed_xT[0],
        "x_scales": packed_xT[1],
        "w1_words": packed_w1[0],
        "w1_scales": packed_w1[1],
        "gn": (np.random.uniform(0.5, 1.5, (H, 1)) * u[:, None]).astype(np.float32),
        "w2_words": packed_w2[0],
        "w2_scales": packed_w2[1],
        "offs": striped(np.random.permutation(T)[:S]),
        "pos": striped8(np.stack([np.random.permutation(S) for _ in range(8)])),
        "neg": striped8(np.stack([np.random.permutation(S) for _ in range(8)])),
    }


def reference(x_words, x_scales, w1_words, w1_scales, gn, w2_words, w2_scales, offs, pos, neg):
    xq = unpack_weight(x_words, x_scales)[:, unstriped(offs)]
    y = unpack_weight(w1_words, w1_scales).T @ xq
    dp = np.abs(y - (y[np.arange(H)[:, None], runs(pos, H)]))
    dn = np.abs(y - (y[np.arange(H)[:, None], runs(neg, H)]))
    z = f64(gn) * (relu(dp - dn + 0.5) * sigmoid(dp))
    out_0 = unpack_weight(w2_words, w2_scales).T @ mxq(z, 0, "e4m3")
    return (out_0,) + planes(out_0)

@@ -1,0 +1,220 @@
+from contextlib import ExitStack
+
+import concourse.mybir as mybir
+
+F32 = mybir.dt.float32
+BF16 = mybir.dt.bfloat16
+I32 = mybir.dt.int32
+U32 = mybir.dt.uint32
+U16 = mybir.dt.uint16
+U8 = mybir.dt.uint8
+FP8X4 = mybir.dt.float8_e4m3fn_x4
+ALU = mybir.AluOpType
+ACT = mybir.ActivationFunctionType
+
+P = 128
+PACK = 4
+T, S, H, N, K = 2048, 512, 512, 512, 512
+HALF = 256
+CHUNK = 128
+FLOPS = 2 * K * H * S + 2 * H * N * S
+
+
+def tile_picked_triplet8_none_po_kernel(
+    tc, x_words, x_scales, w1_words, w1_scales, gn, w2_words, w2_scales, offs, pos, neg, out_0, out_1, out_2
+):
+    nc = tc.nc
+    chunks = S // CHUNK
+    with ExitStack() as ctx:
+        held = ctx.enter_context(tc.tile_pool(name="held", bufs=1))
+        ring = ctx.enter_context(tc.tile_pool(name="ring", bufs=2))
+        psum = ctx.enter_context(tc.psum_pool(name="psum", bufs=1))
+
+        def words_view(words):
+            return words[0].rearrange("p n t -> p (n t)").bitcast(I32)
+
+        def load_scale_rows(queue, plane, scales, quadrants=range(4)):
+            for q in quadrants:
+                queue.dma_start(out=plane[32 * q : 32 * q + 4, :].bitcast(I32), in_=scales[0, 4 * q : 4 * q + 4, :].bitcast(I32))
+
+        offs_t = held.tile([P, S // 16], U16, name="offs_t")
+        pos_t = held.tile([P, S // 16], U16, name="pos_t")
+        neg_t = held.tile([P, S // 16], U16, name="neg_t")
+        xw = held.tile([P, T], I32, name="xw", align_bytes=64)
+        xs = held.tile([P, T], U8, name="xs", align_bytes=64)
+        w1w = held.tile([P, H], I32, name="w1w", align_bytes=64)
+        w1s = held.tile([P, H], U8, name="w1s", align_bytes=64)
+        w2w = held.tile([P, N], I32, name="w2w", align_bytes=64)
+        w2s = held.tile([P, N], U8, name="w2s", align_bytes=64)
+        gain = held.tile([P, PACK], F32, name="gain")
+        warm = held.tile([P, 2], F32, name="warm")
+
+        nc.vector.memset(xs[:].bitcast(I32), 0)
+        nc.vector.memset(warm[:, 0:1], 0.0)
+        nc.gpsimd.memset(w1s[:].bitcast(I32), 0)
+        nc.gpsimd.memset(w2s[:].bitcast(I32), 0)
+        nc.scalar.activation(warm[:, 1:2], warm[:, 0:1], ACT.Sigmoid)
+
+        nc.sync.dma_start(offs_t[:], offs)
+        nc.sync.dma_start(out=xw[:], in_=words_view(x_words))
+        load_scale_rows(nc.sync, xs, x_scales)
+        nc.sync.dma_start(out=w1w[:], in_=words_view(w1_words))
+        load_scale_rows(nc.sync, w1s, w1_scales, range(2))
+        load_scale_rows(nc.gpsimd, w1s, w1_scales, range(2, 4))
+        nc.sync.dma_start(pos_t[:], pos)
+        nc.sync.dma_start(neg_t[:], neg)
+        nc.sync.dma_start(out=gain[:], in_=gn.rearrange("(p t) o -> p (t o)", t=PACK))
+        nc.sync.dma_start(out=w2w[:], in_=words_view(w2_words))
+        load_scale_rows(nc.sync, w2s, w2_scales)
+
+        def deal(name, words, plane):
+            dealt_words = held.tile([P, H], U32, name=name + "_dw", align_bytes=64)
+            dealt_plane = held.tile([P, H], U8, name=name + "_ds", align_bytes=64)
+            nc.vector.tensor_copy(
+                out=dealt_words[:].rearrange("p (t c i) -> p c t i", t=PACK, i=4),
+                in_=words[:].bitcast(U32).rearrange("p (c i t) -> p c t i", t=PACK, i=4),
+            )
+            nc.vector.tensor_copy(
+                out=dealt_plane[:].rearrange("p (t c i) -> p c t i", t=PACK, i=16),
+                in_=plane[:].rearrange("p (c i t) -> p c t i", t=PACK, i=16),
+            )
+            return dealt_words, dealt_plane
+
+        xg = held.tile([P, S], U32, name="xg", align_bytes=64)
+        xgs = held.tile([P, S], U8, name="xgs", align_bytes=64)
+
+        def pick(h):
+            cols = slice(h * HALF, (h + 1) * HALF)
+            ocols = slice(h * HALF // 16, (h + 1) * HALF // 16)
+            nc.vector.tensor_copy(out=xgs[:, cols], in_=xs[:].indirect(offs_t[:, ocols]))
+            nc.vector.tensor_copy(out=xg[:, cols], in_=xw[:].bitcast(U32).indirect(offs_t[:, ocols]))
+
+        win = [held.tile([P, S], F32, name="win%d" % t, align_bytes=64) for t in range(PACK)]
+        own_first = held.tile([P, PACK, CHUNK], F32, name="own_first", align_bytes=64)
+        own_rest = [held.tile([P, S - CHUNK], F32, name="own_rest%d" % t, align_bytes=64) for t in range(PACK)]
+
+        def project(h):
+            cols = slice(h * HALF, (h + 1) * HALF)
+            for tp in range(2):
+                bank = psum.tile([P, 2, HALF], F32, name="ybank%d" % (2 * h + tp))
+                for e in range(2):
+                    t = 2 * tp + e
+                    nc.tensor.matmul_mx(
+                        out=bank[:, e, :],
+                        lhsT=w1d[:, t * P : (t + 1) * P].bitcast(FP8X4),
+                        lhsT_scale=w1sd[:, t * P : (t + 1) * P],
+                        rhs=xg[:, cols].bitcast(FP8X4),
+                        rhs_scale=xgs[:, cols],
+                        start=True,
+                        stop=True,
+                    )
+                for e in range(2):
+                    nc.scalar.copy(out=win[2 * tp + e][:, cols], in_=bank[:, e, :])
+                if h == 0:
+                    nc.scalar.copy(out=own_first[:, 2 * tp : 2 * tp + 2, :], in_=bank[:, :, 0:CHUNK])
+
+        pick(0)
+        w1d, w1sd = deal("w1", w1w, w1s)
+        project(0)
+        pick(1)
+        project(1)
+        for t in range(PACK):
+            nc.sync.dma_start(out=own_rest[t][:], in_=win[t][:, CHUNK:])
+        w2d, w2sd = deal("w2", w2w, w2s)
+
+        zc = held.tile([P, S], U32, name="zc", align_bytes=64)
+        zs = held.tile([P, S], U8, name="zs", align_bytes=64)
+        oc = held.tile([P, S], I32, name="oc", align_bytes=64)
+        osc = held.tile([P, S], U8, name="osc", align_bytes=64)
+        out_rows = out_0.rearrange("(p t) j -> p t j", t=PACK)
+        out_words = words_view(out_1)
+        state = {}
+
+        def fetch(c, lists, name):
+            diff = ring.tile([P, PACK, CHUNK], F32, name=name, align_bytes=64)
+            ocols = slice(c * CHUNK // 16, (c + 1) * CHUNK // 16)
+            for t in range(PACK):
+                own = own_first[:, t, :] if c == 0 else own_rest[t][:, (c - 1) * CHUNK : c * CHUNK]
+                nc.vector.tensor_tensor(diff[:, t, :], win[t][:].indirect(lists[:, ocols]), own, ALU.subtract)
+            return diff
+
+        def fetch_pos(c):
+            a = fetch(c, pos_t, "a")
+            dp = ring.tile([P, PACK, CHUNK], F32, name="dp", align_bytes=64)
+            sig = ring.tile([P, PACK, CHUNK], F32, name="sig", align_bytes=64)
+            nc.scalar.activation(dp[:], a[:], ACT.Abs)
+            nc.scalar.activation(sig[:], dp[:], ACT.Sigmoid)
+            state[("dp", c)] = dp
+            state[("sig", c)] = sig
+
+        def fetch_neg(c):
+            b = fetch(c, neg_t, "b")
+            dn = ring.tile([P, PACK, CHUNK], F32, name="dn", align_bytes=64)
+            nc.scalar.activation(dn[:], b[:], ACT.Abs)
+            state[("dn", c)] = dn
+
+        def margin(c):
+            x = ring.tile([P, PACK, CHUNK], F32, name="x", align_bytes=64)
+            nc.vector.scalar_tensor_tensor(x[:], state[("dp", c)][:], 0.5, state[("dn", c)][:], ALU.add, ALU.subtract)
+            state[("x", c)] = x
+
+        def gained(c):
+            r = ring.tile([P, PACK, CHUNK], F32, name="r", align_bytes=64)
+            for t in range(PACK):
+                nc.vector.tensor_scalar(r[:, t, :], state[("x", c)][:, t, :], 0.0, gain[:, t : t + 1], ALU.max, ALU.mult)
+            state[("r", c)] = r
+
+        def weave(c):
+            z = ring.tile([P, CHUNK, PACK], BF16, name="z", align_bytes=64)
+            nc.vector.tensor_tensor(
+                z[:].rearrange("p (c i) t -> p c t i", i=4),
+                state[("r", c)][:].rearrange("p t (c i) -> p c t i", i=4),
+                state[("sig", c)][:].rearrange("p t (c i) -> p c t i", i=4),
+                ALU.mult,
+            )
+            state[("z", c)] = z
+
+        def second(c):
+            cols = slice(c * CHUNK, (c + 1) * CHUNK)
+            nc.vector.quantize_mx(out=zc[:, cols].bitcast(FP8X4), scales=zs[:, cols], in_=state[("z", c)][:].rearrange("p j t -> p (j t)"))
+            bank = psum.tile([P, PACK, CHUNK], F32, name="obank%d" % c)
+            for t in range(PACK):
+                nc.tensor.matmul_mx(
+                    out=bank[:, t, :],
+                    lhsT=w2d[:, t * P : (t + 1) * P].bitcast(FP8X4),
+                    lhsT_scale=w2sd[:, t * P : (t + 1) * P],
+                    rhs=zc[:, cols].bitcast(FP8X4),
+                    rhs_scale=zs[:, cols],
+                    start=True,
+                    stop=True,
+                )
+            ob = ring.tile([P, CHUNK, PACK], BF16, name="ob", align_bytes=64)
+            of = ring.tile([P, PACK, CHUNK], F32, name="of", align_bytes=64, bufs=4)
+            nc.scalar.copy(out=ob[:], in_=bank[:].rearrange("p t j -> p j t"))
+            nc.scalar.copy(out=of[:], in_=bank[:])
+            nc.sync.dma_start(out=out_rows[:, :, cols], in_=of[:])
+            state[("ob", c)] = ob
+
+        def hand_on(c):
+            cols = slice(c * CHUNK, (c + 1) * CHUNK)
+            nc.vector.quantize_mx(out=oc[:, cols].bitcast(FP8X4), scales=osc[:, cols], in_=state[("ob", c)][:].rearrange("p j t -> p (j t)"))
+            nc.sync.dma_start(out=out_words[:, cols], in_=oc[:, cols])
+
+        fetch_pos(0)
+        fetch_neg(0)
+        for c in range(chunks):
+            more = c + 1 < chunks
+            if more:
+                fetch_pos(c + 1)
+            margin(c)
+            if c > 0:
+                hand_on(c - 1)
+            gained(c)
+            if more:
+                fetch_neg(c + 1)
+            weave(c)
+            second(c)
+        hand_on(chunks - 1)
+        for q in range(4):
+            queue = nc.scalar if q % 2 else nc.sync
+            queue.dma_start(out=out_2[0, 4 * q : 4 * q + 4, :].bitcast(I32), in_=osc[32 * q : 32 * q + 4, :].bitcast(I32))

@@ -49,78 +49,83 @@ def tile_picked_triplet8_none_po_kernel(
         gain = held.tile([P, PACK], F32, name="gain")
         warm = held.tile([P, 2], F32, name="warm")
 
-        nc.vector.memset(xs[:].bitcast(I32), 0)
-        nc.vector.memset(warm[:, 0:1], 0.0)
+        nc.vector.memset(xs[:, 0 : T // 2].bitcast(I32), 0)
+        nc.gpsimd.memset(xs[:, T // 2 : T].bitcast(I32), 0)
         nc.gpsimd.memset(w1s[:].bitcast(I32), 0)
         nc.gpsimd.memset(w2s[:].bitcast(I32), 0)
+        nc.vector.memset(warm[:, 0:1], 0.0)
         nc.scalar.activation(warm[:, 1:2], warm[:, 0:1], ACT.Sigmoid)
 
         nc.sync.dma_start(offs_t[:], offs)
-        nc.sync.dma_start(out=xw[:], in_=words_view(x_words))
-        load_scale_rows(nc.sync, xs, x_scales)
         nc.sync.dma_start(out=w1w[:], in_=words_view(w1_words))
-        load_scale_rows(nc.sync, w1s, w1_scales, range(2))
-        load_scale_rows(nc.gpsimd, w1s, w1_scales, range(2, 4))
         nc.sync.dma_start(pos_t[:], pos)
+        load_scale_rows(nc.sync, xs, x_scales)
+        nc.sync.dma_start(out=xw[:], in_=words_view(x_words))
+        load_scale_rows(nc.sync, w1s, w1_scales)
         nc.sync.dma_start(neg_t[:], neg)
-        nc.sync.dma_start(out=gain[:], in_=gn.rearrange("(p t) o -> p (t o)", t=PACK))
         nc.sync.dma_start(out=w2w[:], in_=words_view(w2_words))
         load_scale_rows(nc.sync, w2s, w2_scales)
+        nc.sync.dma_start(out=gain[:], in_=gn.rearrange("(p t) o -> p (t o)", t=PACK))
 
-        def deal(name, words, plane):
-            dealt_words = held.tile([P, H], U32, name=name + "_dw", align_bytes=64)
-            dealt_plane = held.tile([P, H], U8, name=name + "_ds", align_bytes=64)
+        def deal_words(name, words):
+            dealt = held.tile([P, H], U32, name=name, align_bytes=64)
             nc.vector.tensor_copy(
-                out=dealt_words[:].rearrange("p (t c i) -> p c t i", t=PACK, i=4),
+                out=dealt[:].rearrange("p (t c i) -> p c t i", t=PACK, i=4),
                 in_=words[:].bitcast(U32).rearrange("p (c i t) -> p c t i", t=PACK, i=4),
             )
-            nc.vector.tensor_copy(
-                out=dealt_plane[:].rearrange("p (t c i) -> p c t i", t=PACK, i=16),
-                in_=plane[:].rearrange("p (c i t) -> p c t i", t=PACK, i=16),
-            )
-            return dealt_words, dealt_plane
+            return dealt
 
+        def deal_bytes(dealt, plane, first, last):
+            nc.vector.tensor_copy(
+                out=dealt[:].rearrange("p (t c i) -> p c t i", t=PACK, i=16)[:, :, first:last, :],
+                in_=plane[:].rearrange("p (c i t) -> p c t i", t=PACK, i=16)[:, :, first:last, :],
+            )
+
+        w1sd = held.tile([P, H], U8, name="w1sd", align_bytes=64)
+        w2sd = held.tile([P, N], U8, name="w2sd", align_bytes=64)
         xg = held.tile([P, S], U32, name="xg", align_bytes=64)
         xgs = held.tile([P, S], U8, name="xgs", align_bytes=64)
 
-        def pick(h):
-            cols = slice(h * HALF, (h + 1) * HALF)
-            ocols = slice(h * HALF // 16, (h + 1) * HALF // 16)
-            nc.vector.tensor_copy(out=xgs[:, cols], in_=xs[:].indirect(offs_t[:, ocols]))
-            nc.vector.tensor_copy(out=xg[:, cols], in_=xw[:].bitcast(U32).indirect(offs_t[:, ocols]))
+        def half(h):
+            return slice(h * HALF, (h + 1) * HALF), slice(h * HALF // 16, (h + 1) * HALF // 16)
 
         win = [held.tile([P, S], F32, name="win%d" % t, align_bytes=64) for t in range(PACK)]
-        own_first = held.tile([P, PACK, CHUNK], F32, name="own_first", align_bytes=64)
-        own_rest = [held.tile([P, S - CHUNK], F32, name="own_rest%d" % t, align_bytes=64) for t in range(PACK)]
+        own = [[held.tile([P, HALF], F32, name="own%d_%d" % (h, t), align_bytes=64) for t in range(PACK)] for h in range(2)]
 
-        def project(h):
-            cols = slice(h * HALF, (h + 1) * HALF)
-            for tp in range(2):
-                bank = psum.tile([P, 2, HALF], F32, name="ybank%d" % (2 * h + tp))
-                for e in range(2):
-                    t = 2 * tp + e
-                    nc.tensor.matmul_mx(
-                        out=bank[:, e, :],
-                        lhsT=w1d[:, t * P : (t + 1) * P].bitcast(FP8X4),
-                        lhsT_scale=w1sd[:, t * P : (t + 1) * P],
-                        rhs=xg[:, cols].bitcast(FP8X4),
-                        rhs_scale=xgs[:, cols],
-                        start=True,
-                        stop=True,
-                    )
-                for e in range(2):
-                    nc.scalar.copy(out=win[2 * tp + e][:, cols], in_=bank[:, e, :])
-                if h == 0:
-                    nc.scalar.copy(out=own_first[:, 2 * tp : 2 * tp + 2, :], in_=bank[:, :, 0:CHUNK])
+        def project(t, h):
+            cols = half(h)[0]
+            bank = psum.tile([P, S], F32, name="bank%d" % (2 * t + h))
+            nc.tensor.matmul_mx(
+                out=bank[:, 0:HALF],
+                lhsT=w1d[:, t * P : (t + 1) * P].bitcast(FP8X4),
+                lhsT_scale=w1sd[:, t * P : (t + 1) * P],
+                rhs=xg[:, cols].bitcast(FP8X4),
+                rhs_scale=xgs[:, cols],
+                start=True,
+                stop=True,
+            )
+            if t == 0 and h == 1:
+                nc.vector.tensor_copy(out=win[t][:, cols], in_=bank[:, 0:HALF])
+            else:
+                nc.scalar.copy(out=win[t][:, cols], in_=bank[:, 0:HALF])
+            if h == 0:
+                nc.scalar.copy(out=own[0][t][:], in_=bank[:, 0:HALF])
+            else:
+                nc.sync.dma_start(out=own[h][t][:], in_=win[t][:, cols])
 
-        pick(0)
-        w1d, w1sd = deal("w1", w1w, w1s)
-        project(0)
-        pick(1)
-        project(1)
+        nc.vector.tensor_copy(out=xgs[:], in_=xs[:].indirect(offs_t[:]))
+        w1d = deal_words("w1d", w1w)
+        for h in range(2):
+            cols, ocols = half(h)
+            nc.vector.tensor_copy(out=xg[:, cols], in_=xw[:].bitcast(U32).indirect(offs_t[:, ocols]))
+            if h == 0:
+                deal_bytes(w1sd, w1s, 0, 1)
+        deal_bytes(w1sd, w1s, 1, PACK)
         for t in range(PACK):
-            nc.sync.dma_start(out=own_rest[t][:], in_=win[t][:, CHUNK:])
-        w2d, w2sd = deal("w2", w2w, w2s)
+            for h in range(2):
+                project(t, h)
+        w2d = deal_words("w2d", w2w)
+        deal_bytes(w2sd, w2s, 0, PACK)
 
         zc = held.tile([P, S], U32, name="zc", align_bytes=64)
         zs = held.tile([P, S], U8, name="zs", align_bytes=64)
@@ -128,59 +133,49 @@ def tile_picked_triplet8_none_po_kernel(
         osc = held.tile([P, S], U8, name="osc", align_bytes=64)
         out_rows = out_0.rearrange("(p t) j -> p t j", t=PACK)
         out_words = words_view(out_1)
+        diff = {(n, h): held.tile([P, PACK, HALF], F32, name="diff%s%d" % (n, h), align_bytes=64) for n in "pn" for h in range(2)}
+        dist = {(n, h): held.tile([P, HALF, PACK], F32, name="dist%s%d" % (n, h), align_bytes=64) for n in "pn" for h in range(2)}
+        sig = [held.tile([P, HALF, PACK], F32, name="sig%d" % h, align_bytes=64) for h in range(2)]
+        lists = {"p": pos_t, "n": neg_t}
+
+        def fetch(n, h, t):
+            nc.vector.tensor_tensor(diff[n, h][:, t, :], win[t][:].indirect(lists[n][:, half(h)[1]]), own[h][t][:], ALU.subtract)
+
+        def distance(n, h, cols):
+            nc.scalar.activation(dist[n, h][:, cols, :], diff[n, h][:, :, cols].rearrange("p t j -> p j t"), ACT.Abs)
+
+        def gate(h):
+            nc.scalar.activation(sig[h][:], dist["p", h][:], ACT.Sigmoid)
+
         state = {}
 
-        def fetch(c, lists, name):
-            diff = ring.tile([P, PACK, CHUNK], F32, name=name, align_bytes=64)
-            ocols = slice(c * CHUNK // 16, (c + 1) * CHUNK // 16)
-            for t in range(PACK):
-                own = own_first[:, t, :] if c == 0 else own_rest[t][:, (c - 1) * CHUNK : c * CHUNK]
-                nc.vector.tensor_tensor(diff[:, t, :], win[t][:].indirect(lists[:, ocols]), own, ALU.subtract)
-            return diff
-
-        def fetch_pos(c):
-            a = fetch(c, pos_t, "a")
-            dp = ring.tile([P, PACK, CHUNK], F32, name="dp", align_bytes=64)
-            sig = ring.tile([P, PACK, CHUNK], F32, name="sig", align_bytes=64)
-            nc.scalar.activation(dp[:], a[:], ACT.Abs)
-            nc.scalar.activation(sig[:], dp[:], ACT.Sigmoid)
-            state[("dp", c)] = dp
-            state[("sig", c)] = sig
-
-        def fetch_neg(c):
-            b = fetch(c, neg_t, "b")
-            dn = ring.tile([P, PACK, CHUNK], F32, name="dn", align_bytes=64)
-            nc.scalar.activation(dn[:], b[:], ACT.Abs)
-            state[("dn", c)] = dn
+        def part(c):
+            return c // 2, slice(c % 2 * CHUNK, (c % 2 + 1) * CHUNK)
 
         def margin(c):
-            x = ring.tile([P, PACK, CHUNK], F32, name="x", align_bytes=64)
-            nc.vector.scalar_tensor_tensor(x[:], state[("dp", c)][:], 0.5, state[("dn", c)][:], ALU.add, ALU.subtract)
-            state[("x", c)] = x
+            h, cols = part(c)
+            x = ring.tile([P, CHUNK, PACK], F32, name="x", align_bytes=64)
+            nc.vector.scalar_tensor_tensor(x[:], dist["p", h][:, cols, :], 0.5, dist["n", h][:, cols, :], ALU.add, ALU.subtract)
+            state["x", c] = x
+
+        def gated(c):
+            h, cols = part(c)
+            w = ring.tile([P, CHUNK, PACK], F32, name="w", align_bytes=64)
+            nc.vector.scalar_tensor_tensor(w[:], state["x", c][:], 0.0, sig[h][:, cols, :], ALU.max, ALU.mult)
+            state["w", c] = w
 
         def gained(c):
-            r = ring.tile([P, PACK, CHUNK], F32, name="r", align_bytes=64)
-            for t in range(PACK):
-                nc.vector.tensor_scalar(r[:, t, :], state[("x", c)][:, t, :], 0.0, gain[:, t : t + 1], ALU.max, ALU.mult)
-            state[("r", c)] = r
-
-        def weave(c):
             z = ring.tile([P, CHUNK, PACK], BF16, name="z", align_bytes=64)
-            nc.vector.tensor_tensor(
-                z[:].rearrange("p (c i) t -> p c t i", i=4),
-                state[("r", c)][:].rearrange("p t (c i) -> p c t i", i=4),
-                state[("sig", c)][:].rearrange("p t (c i) -> p c t i", i=4),
-                ALU.mult,
-            )
-            state[("z", c)] = z
+            nc.vector.tensor_tensor(z[:], state["w", c][:], gain[:].unsqueeze(1).to_broadcast([P, CHUNK, PACK]), ALU.mult)
+            state["z", c] = z
 
         def second(c):
             cols = slice(c * CHUNK, (c + 1) * CHUNK)
-            nc.vector.quantize_mx(out=zc[:, cols].bitcast(FP8X4), scales=zs[:, cols], in_=state[("z", c)][:].rearrange("p j t -> p (j t)"))
-            bank = psum.tile([P, PACK, CHUNK], F32, name="obank%d" % c)
+            nc.vector.quantize_mx(out=zc[:, cols].bitcast(FP8X4), scales=zs[:, cols], in_=state["z", c][:].rearrange("p j t -> p (j t)"))
+            bank = psum.tile([P, S], F32, name="bank%d" % c)
             for t in range(PACK):
                 nc.tensor.matmul_mx(
-                    out=bank[:, t, :],
+                    out=bank[:, t * CHUNK : (t + 1) * CHUNK],
                     lhsT=w2d[:, t * P : (t + 1) * P].bitcast(FP8X4),
                     lhsT_scale=w2sd[:, t * P : (t + 1) * P],
                     rhs=zc[:, cols].bitcast(FP8X4),
@@ -188,33 +183,41 @@ def tile_picked_triplet8_none_po_kernel(
                     start=True,
                     stop=True,
                 )
-            ob = ring.tile([P, CHUNK, PACK], BF16, name="ob", align_bytes=64)
+            ob = ring.tile([P, CHUNK, PACK], BF16, name="ob", align_bytes=64, bufs=4)
             of = ring.tile([P, PACK, CHUNK], F32, name="of", align_bytes=64, bufs=4)
-            nc.scalar.copy(out=ob[:], in_=bank[:].rearrange("p t j -> p j t"))
-            nc.scalar.copy(out=of[:], in_=bank[:])
+            nc.scalar.copy(out=ob[:], in_=bank[:].rearrange("p (t j) -> p j t", t=PACK))
+            nc.scalar.copy(out=of[:], in_=bank[:].rearrange("p (t j) -> p t j", t=PACK))
             nc.sync.dma_start(out=out_rows[:, :, cols], in_=of[:])
-            state[("ob", c)] = ob
+            state["ob", c] = ob
 
         def hand_on(c):
             cols = slice(c * CHUNK, (c + 1) * CHUNK)
-            nc.vector.quantize_mx(out=oc[:, cols].bitcast(FP8X4), scales=osc[:, cols], in_=state[("ob", c)][:].rearrange("p j t -> p (j t)"))
+            nc.vector.quantize_mx(out=oc[:, cols].bitcast(FP8X4), scales=osc[:, cols], in_=state["ob", c][:].rearrange("p j t -> p (j t)"))
             nc.sync.dma_start(out=out_words[:, cols], in_=oc[:, cols])
 
-        fetch_pos(0)
-        fetch_neg(0)
-        for c in range(chunks):
-            more = c + 1 < chunks
-            if more:
-                fetch_pos(c + 1)
-            margin(c)
-            if c > 0:
-                hand_on(c - 1)
-            gained(c)
-            if more:
-                fetch_neg(c + 1)
-            weave(c)
-            second(c)
-        hand_on(chunks - 1)
+        whole = slice(0, HALF)
+        for t in range(PACK):
+            fetch("p", 0, t)
+            fetch("n", 0, t)
+        distance("p", 0, whole)
+        distance("n", 0, whole)
+        gate(0)
+        for t in range(PACK):
+            fetch("p", 1, t)
+        distance("p", 1, whole)
+        gate(1)
+        for t in range(PACK):
+            fetch("n", 1, t)
+        for c in (2, 3):
+            distance("n", 1, part(c)[1])
+        steps = (margin, gated, gained, second)
+        for turn in range(2 * chunks + len(steps)):
+            for c in range(chunks):
+                stage = turn - 2 * c
+                if 0 <= stage < len(steps):
+                    steps[stage](c)
+                if stage == len(steps) + 1:
+                    hand_on(c)
         for q in range(4):
             queue = nc.scalar if q % 2 else nc.sync
             queue.dma_start(out=out_2[0, 4 * q : 4 * q + 4, :].bitcast(I32), in_=osc[32 * q : 32 * q + 4, :].bitcast(I32))

@@ -17,6 +17,7 @@ PACK = 4
 T, S, H, N, K = 2048, 512, 512, 512, 512
 HALF = 256
 CHUNK = 128
+LATE = 2
 FLOPS = 2 * K * H * S + 2 * H * N * S
 
 
@@ -82,7 +83,6 @@ def tile_picked_triplet8_none_po_kernel(
             )
 
         w1sd = held.tile([P, H], U8, name="w1sd", align_bytes=64)
-        w2sd = held.tile([P, N], U8, name="w2sd", align_bytes=64)
         xg = held.tile([P, S], U32, name="xg", align_bytes=64)
         xgs = held.tile([P, S], U8, name="xgs", align_bytes=64)
 
@@ -90,7 +90,7 @@ def tile_picked_triplet8_none_po_kernel(
             return slice(h * HALF, (h + 1) * HALF), slice(h * HALF // 16, (h + 1) * HALF // 16)
 
         win = [held.tile([P, S], F32, name="win%d" % t, align_bytes=64) for t in range(PACK)]
-        own = [[held.tile([P, HALF], F32, name="own%d_%d" % (h, t), align_bytes=64) for t in range(PACK)] for h in range(2)]
+        own = [[held.tile([P, HALF], F32, name="own%d_%d" % (h, t), tag="own%d_%d" % (h, t), align_bytes=64) for t in range(PACK)] for h in range(2)]
 
         def project(t, h):
             cols = half(h)[0]
@@ -125,7 +125,6 @@ def tile_picked_triplet8_none_po_kernel(
             for h in range(2):
                 project(t, h)
         w2d = deal_words("w2d", w2w)
-        deal_bytes(w2sd, w2s, 0, PACK)
 
         zc = held.tile([P, S], U32, name="zc", align_bytes=64)
         zs = held.tile([P, S], U8, name="zs", align_bytes=64)
@@ -133,19 +132,23 @@ def tile_picked_triplet8_none_po_kernel(
         osc = held.tile([P, S], U8, name="osc", align_bytes=64)
         out_rows = out_0.rearrange("(p t) j -> p t j", t=PACK)
         out_words = words_view(out_1)
-        diff = {(n, h): held.tile([P, PACK, HALF], F32, name="diff%s%d" % (n, h), align_bytes=64) for n in "pn" for h in range(2)}
-        dist = {(n, h): held.tile([P, HALF, PACK], F32, name="dist%s%d" % (n, h), align_bytes=64) for n in "pn" for h in range(2)}
-        sig = [held.tile([P, HALF, PACK], F32, name="sig%d" % h, align_bytes=64) for h in range(2)]
+        def rows(name, tag):
+            return held.tile([P, PACK, HALF], F32, name=name, tag=tag, align_bytes=64)
+
+        diff = {(n, h): rows("diff%s%d" % (n, h), "diff%s%d" % (n, h)) for n in "pn" for h in range(2)}
+        dist = {(n, h): rows("dist%s%d" % (n, h), "dist%s%d" % (n, h)) for n in "pn" for h in range(2)}
+        sig = [rows("sig%d" % h, "sig%d" % h) for h in range(2)]
         lists = {"p": pos_t, "n": neg_t}
 
         def fetch(n, h, t):
             nc.vector.tensor_tensor(diff[n, h][:, t, :], win[t][:].indirect(lists[n][:, half(h)[1]]), own[h][t][:], ALU.subtract)
 
-        def distance(n, h, cols):
-            nc.scalar.activation(dist[n, h][:, cols, :], diff[n, h][:, :, cols].rearrange("p t j -> p j t"), ACT.Abs)
-
-        def gate(h):
-            nc.scalar.activation(sig[h][:], dist["p", h][:], ACT.Sigmoid)
+        def measure(n, h, first, last):
+            nc.scalar.activation(dist[n, h][:, first:last, :], diff[n, h][:, first:last, :], ACT.Abs)
+            if n == "p":
+                nc.scalar.activation(diff[n, h][:, first:last, :], dist[n, h][:, first:last, :], ACT.Sigmoid)
+                for t in range(first, last):
+                    nc.scalar.activation(sig[h][:, t, :], diff[n, h][:, t, :], ACT.Copy, scale=gain[:, t : t + 1])
 
         state = {}
 
@@ -154,70 +157,93 @@ def tile_picked_triplet8_none_po_kernel(
 
         def margin(c):
             h, cols = part(c)
-            x = ring.tile([P, CHUNK, PACK], F32, name="x", align_bytes=64)
-            nc.vector.scalar_tensor_tensor(x[:], dist["p", h][:, cols, :], 0.5, dist["n", h][:, cols, :], ALU.add, ALU.subtract)
+            x = ring.tile([P, PACK, CHUNK], F32, name="x", align_bytes=64, bufs=4)
+            nc.vector.scalar_tensor_tensor(x[:], dist["p", h][:, :, cols], 0.5, dist["n", h][:, :, cols], ALU.add, ALU.subtract)
             state["x", c] = x
 
         def gated(c):
             h, cols = part(c)
-            w = ring.tile([P, CHUNK, PACK], F32, name="w", align_bytes=64)
-            nc.vector.scalar_tensor_tensor(w[:], state["x", c][:], 0.0, sig[h][:, cols, :], ALU.max, ALU.mult)
-            state["w", c] = w
+            zn = ring.tile([P, PACK, CHUNK], BF16, name="zn", align_bytes=64, bufs=4)
+            nc.vector.scalar_tensor_tensor(zn[:], state["x", c][:], 0.0, sig[h][:, :, cols], ALU.max, ALU.mult)
+            state["zn", c] = zn
 
-        def gained(c):
-            z = ring.tile([P, CHUNK, PACK], BF16, name="z", align_bytes=64)
-            nc.vector.tensor_tensor(z[:], state["w", c][:], gain[:].unsqueeze(1).to_broadcast([P, CHUNK, PACK]), ALU.mult)
+        def weave(c):
+            z = ring.tile([P, CHUNK, PACK], BF16, name="z", align_bytes=64, bufs=4)
+            if c < LATE:
+                nc.scalar.copy(out=z[:], in_=state["zn", c][:].rearrange("p t j -> p j t"))
+            else:
+                nc.vector.tensor_copy(out=z[:], in_=state["zn", c][:].rearrange("p t j -> p j t"))
             state["z", c] = z
 
         def second(c):
             cols = slice(c * CHUNK, (c + 1) * CHUNK)
             nc.vector.quantize_mx(out=zc[:, cols].bitcast(FP8X4), scales=zs[:, cols], in_=state["z", c][:].rearrange("p j t -> p (j t)"))
-            bank = psum.tile([P, S], F32, name="bank%d" % c)
-            for t in range(PACK):
-                nc.tensor.matmul_mx(
-                    out=bank[:, t * CHUNK : (t + 1) * CHUNK],
-                    lhsT=w2d[:, t * P : (t + 1) * P].bitcast(FP8X4),
-                    lhsT_scale=w2sd[:, t * P : (t + 1) * P],
-                    rhs=zc[:, cols].bitcast(FP8X4),
-                    rhs_scale=zs[:, cols],
-                    start=True,
-                    stop=True,
-                )
             ob = ring.tile([P, CHUNK, PACK], BF16, name="ob", align_bytes=64, bufs=4)
             of = ring.tile([P, PACK, CHUNK], F32, name="of", align_bytes=64, bufs=4)
-            nc.scalar.copy(out=ob[:], in_=bank[:].rearrange("p (t j) -> p j t", t=PACK))
-            nc.scalar.copy(out=of[:], in_=bank[:].rearrange("p (t j) -> p t j", t=PACK))
-            nc.sync.dma_start(out=out_rows[:, :, cols], in_=of[:])
+            last = c + 1 == chunks
+            for first, end in ((0, 2), (2, 4)) if last else ((0, 4),):
+                bank = psum.tile([P, S], F32, name="bank%d" % (c + first // 2))
+                for t in range(first, end):
+                    nc.tensor.matmul_mx(
+                        out=bank[:, t * CHUNK : (t + 1) * CHUNK],
+                        lhsT=w2d[:, t * P : (t + 1) * P].bitcast(FP8X4),
+                        lhsT_scale=w2sd[:, t * P : (t + 1) * P],
+                        rhs=zc[:, cols].bitcast(FP8X4),
+                        rhs_scale=zs[:, cols],
+                        start=True,
+                        stop=True,
+                    )
+                if c < LATE:
+                    nc.scalar.copy(out=ob[:], in_=bank[:].rearrange("p (t j) -> p j t", t=PACK))
+                sums = bank[:].rearrange("p (t j) -> p t j", t=PACK)[:, first:end, :]
+                if first:
+                    nc.vector.tensor_copy(out=of[:, first:end, :], in_=sums)
+                else:
+                    nc.scalar.copy(out=of[:, first:end, :], in_=sums)
+                nc.sync.dma_start(out=out_rows[:, first:end, cols], in_=of[:, first:end, :])
             state["ob", c] = ob
+            state["of", c] = of
 
         def hand_on(c):
             cols = slice(c * CHUNK, (c + 1) * CHUNK)
+            if c >= LATE:
+                nc.vector.tensor_copy(out=state["ob", c][:], in_=state["of", c][:].rearrange("p t j -> p j t"))
             nc.vector.quantize_mx(out=oc[:, cols].bitcast(FP8X4), scales=osc[:, cols], in_=state["ob", c][:].rearrange("p j t -> p (j t)"))
-            nc.sync.dma_start(out=out_words[:, cols], in_=oc[:, cols])
+            if c % 2:
+                nc.sync.dma_start(out=out_words[:, half(c // 2)[0]], in_=oc[:, half(c // 2)[0]])
 
-        whole = slice(0, HALF)
         for t in range(PACK):
             fetch("p", 0, t)
             fetch("n", 0, t)
-        distance("p", 0, whole)
-        distance("n", 0, whole)
-        gate(0)
-        for t in range(PACK):
-            fetch("p", 1, t)
-        distance("p", 1, whole)
-        gate(1)
-        for t in range(PACK):
-            fetch("n", 1, t)
-        for c in (2, 3):
-            distance("n", 1, part(c)[1])
-        steps = (margin, gated, gained, second)
-        for turn in range(2 * chunks + len(steps)):
-            for c in range(chunks):
-                stage = turn - 2 * c
-                if 0 <= stage < len(steps):
-                    steps[stage](c)
-                if stage == len(steps) + 1:
-                    hand_on(c)
+            if t == 0:
+                w2sd = held.tile([P, N], U8, name="w2sd", tag="own0_0", align_bytes=64)
+                deal_bytes(w2sd, w2s, 0, PACK)
+            measure("p", 0, t, t + 1)
+            measure("n", 0, t, t + 1)
+        for n in "pn":
+            for t in range(PACK):
+                fetch(n, 1, t)
+                measure(n, 1, t, t + 1)
+        margin(0)
+        margin(1)
+        gated(0)
+        weave(0)
+        gated(1)
+        weave(1)
+        margin(2)
+        second(0)
+        gated(2)
+        margin(3)
+        second(1)
+        weave(2)
+        gated(3)
+        second(2)
+        weave(3)
+        hand_on(0)
+        second(3)
+        hand_on(1)
+        hand_on(2)
+        hand_on(3)
         for q in range(4):
             queue = nc.scalar if q % 2 else nc.sync
             queue.dma_start(out=out_2[0, 4 * q : 4 * q + 4, :].bitcast(I32), in_=osc[32 * q : 32 * q + 4, :].bitcast(I32))

@@ -108,7 +108,7 @@ def tile_picked_triplet8_none_po_kernel(
                 nc.vector.tensor_copy(out=win[t][:, cols], in_=bank[:, 0:HALF])
             else:
                 nc.scalar.copy(out=win[t][:, cols], in_=bank[:, 0:HALF])
-            if h == 0:
+            if h == 0 and t < 2:
                 nc.scalar.copy(out=own[0][t][:], in_=bank[:, 0:HALF])
             else:
                 nc.sync.dma_start(out=own[h][t][:], in_=win[t][:, cols])
@@ -161,6 +161,12 @@ def tile_picked_triplet8_none_po_kernel(
             nc.vector.scalar_tensor_tensor(x[:], dist["p", h][:, :, cols], 0.5, dist["n", h][:, :, cols], ALU.add, ALU.subtract)
             state["x", c] = x
 
+        def woven(tile):
+            return tile[:].rearrange("p (c i) t -> p c t i", i=4)
+
+        def by_tile(tile):
+            return tile[:].rearrange("p t (c i) -> p c t i", i=4)
+
         def gated(c):
             h, cols = part(c)
             zn = ring.tile([P, PACK, CHUNK], BF16, name="zn", align_bytes=64, bufs=4)
@@ -170,9 +176,9 @@ def tile_picked_triplet8_none_po_kernel(
         def weave(c):
             z = ring.tile([P, CHUNK, PACK], BF16, name="z", align_bytes=64, bufs=4)
             if c < LATE:
-                nc.scalar.copy(out=z[:], in_=state["zn", c][:].rearrange("p t j -> p j t"))
+                nc.scalar.copy(out=woven(z), in_=by_tile(state["zn", c]))
             else:
-                nc.vector.tensor_copy(out=z[:], in_=state["zn", c][:].rearrange("p t j -> p j t"))
+                nc.vector.tensor_copy(out=woven(z), in_=by_tile(state["zn", c]))
             state["z", c] = z
 
         def second(c):
@@ -196,34 +202,33 @@ def tile_picked_triplet8_none_po_kernel(
                 if c < LATE:
                     nc.scalar.copy(out=ob[:], in_=bank[:].rearrange("p (t j) -> p j t", t=PACK))
                 sums = bank[:].rearrange("p (t j) -> p t j", t=PACK)[:, first:end, :]
-                if first:
+                if c == LATE:
                     nc.vector.tensor_copy(out=of[:, first:end, :], in_=sums)
                 else:
                     nc.scalar.copy(out=of[:, first:end, :], in_=sums)
-                nc.sync.dma_start(out=out_rows[:, first:end, cols], in_=of[:, first:end, :])
+            nc.sync.dma_start(out=out_rows[:, :, cols], in_=of[:])
             state["ob", c] = ob
             state["of", c] = of
 
+        def weave_out(c):
+            nc.vector.tensor_copy(out=woven(state["ob", c]), in_=by_tile(state["of", c]))
+
         def hand_on(c):
             cols = slice(c * CHUNK, (c + 1) * CHUNK)
-            if c >= LATE:
-                nc.vector.tensor_copy(out=state["ob", c][:], in_=state["of", c][:].rearrange("p t j -> p j t"))
             nc.vector.quantize_mx(out=oc[:, cols].bitcast(FP8X4), scales=osc[:, cols], in_=state["ob", c][:].rearrange("p j t -> p (j t)"))
             if c % 2:
                 nc.sync.dma_start(out=out_words[:, half(c // 2)[0]], in_=oc[:, half(c // 2)[0]])
 
-        for t in range(PACK):
-            fetch("p", 0, t)
-            fetch("n", 0, t)
-            if t == 0:
-                w2sd = held.tile([P, N], U8, name="w2sd", tag="own0_0", align_bytes=64)
-                deal_bytes(w2sd, w2s, 0, PACK)
-            measure("p", 0, t, t + 1)
-            measure("n", 0, t, t + 1)
-        for n in "pn":
-            for t in range(PACK):
-                fetch(n, 1, t)
-                measure(n, 1, t, t + 1)
+        for first in (0, 2):
+            for h in range(2):
+                for t in (first, first + 1):
+                    fetch("p", h, t)
+                    fetch("n", h, t)
+                    if t == 0 and h == 0:
+                        w2sd = held.tile([P, N], U8, name="w2sd", tag="own0_0", align_bytes=64)
+                        deal_bytes(w2sd, w2s, 0, PACK)
+                    measure("p", h, t, t + 1)
+                    measure("n", h, t, t + 1)
         margin(0)
         margin(1)
         gated(0)
@@ -239,9 +244,11 @@ def tile_picked_triplet8_none_po_kernel(
         gated(3)
         second(2)
         weave(3)
-        hand_on(0)
         second(3)
+        hand_on(0)
         hand_on(1)
+        weave_out(2)
+        weave_out(3)
         hand_on(2)
         hand_on(3)
         for q in range(4):

from contextlib import ExitStack

import concourse.mybir as mybir

F32 = mybir.dt.float32
BF16 = mybir.dt.bfloat16
I32 = mybir.dt.int32
U32 = mybir.dt.uint32
U16 = mybir.dt.uint16
U8 = mybir.dt.uint8
FP8X4 = mybir.dt.float8_e4m3fn_x4
ALU = mybir.AluOpType
ACT = mybir.ActivationFunctionType

P = 128
PACK = 4
T, S, H, N, K = 2048, 512, 512, 512, 512
HALF = 256
CHUNK = 128
LATE = 2
FLOPS = 2 * K * H * S + 2 * H * N * S


def tile_picked_triplet8_none_po_kernel(
    tc, x_words, x_scales, w1_words, w1_scales, gn, w2_words, w2_scales, offs, pos, neg, out_0, out_1, out_2
):
    nc = tc.nc
    chunks = S // CHUNK
    with ExitStack() as ctx:
        held = ctx.enter_context(tc.tile_pool(name="held", bufs=1))
        ring = ctx.enter_context(tc.tile_pool(name="ring", bufs=2))
        psum = ctx.enter_context(tc.psum_pool(name="psum", bufs=1))

        def words_view(words):
            return words[0].rearrange("p n t -> p (n t)").bitcast(I32)

        def load_scale_rows(queue, plane, scales, quadrants=range(4)):
            for q in quadrants:
                queue.dma_start(out=plane[32 * q : 32 * q + 4, :].bitcast(I32), in_=scales[0, 4 * q : 4 * q + 4, :].bitcast(I32))

        offs_t = held.tile([P, S // 16], U16, name="offs_t")
        pos_t = held.tile([P, S // 16], U16, name="pos_t")
        neg_t = held.tile([P, S // 16], U16, name="neg_t")
        xw = held.tile([P, T], I32, name="xw", align_bytes=64)
        xs = held.tile([P, T], U8, name="xs", align_bytes=64)
        w1w = held.tile([P, H], I32, name="w1w", align_bytes=64)
        w1s = held.tile([P, H], U8, name="w1s", align_bytes=64)
        w2w = held.tile([P, N], I32, name="w2w", align_bytes=64)
        w2s = held.tile([P, N], U8, name="w2s", align_bytes=64)
        gain = held.tile([P, PACK], F32, name="gain")
        warm = held.tile([P, 2], F32, name="warm")

        nc.vector.memset(xs[:, 0 : T // 2].bitcast(I32), 0)
        nc.gpsimd.memset(xs[:, T // 2 : T].bitcast(I32), 0)
        nc.gpsimd.memset(w1s[:].bitcast(I32), 0)
        nc.gpsimd.memset(w2s[:].bitcast(I32), 0)
        nc.vector.memset(warm[:, 0:1], 0.0)
        nc.scalar.activation(warm[:, 1:2], warm[:, 0:1], ACT.Sigmoid)

        nc.sync.dma_start(offs_t[:], offs)
        nc.sync.dma_start(out=w1w[:], in_=words_view(w1_words))
        nc.sync.dma_start(pos_t[:], pos)
        load_scale_rows(nc.sync, xs, x_scales)
        nc.sync.dma_start(out=xw[:], in_=words_view(x_words))
        load_scale_rows(nc.sync, w1s, w1_scales)
        nc.sync.dma_start(neg_t[:], neg)
        nc.sync.dma_start(out=w2w[:], in_=words_view(w2_words))
        load_scale_rows(nc.sync, w2s, w2_scales)
        nc.sync.dma_start(out=gain[:], in_=gn.rearrange("(p t) o -> p (t o)", t=PACK))

        def deal_words(name, words):
            dealt = held.tile([P, H], U32, name=name, align_bytes=64)
            nc.vector.tensor_copy(
                out=dealt[:].rearrange("p (t c i) -> p c t i", t=PACK, i=4),
                in_=words[:].bitcast(U32).rearrange("p (c i t) -> p c t i", t=PACK, i=4),
            )
            return dealt

        def deal_bytes(dealt, plane, first, last):
            nc.vector.tensor_copy(
                out=dealt[:].rearrange("p (t c i) -> p c t i", t=PACK, i=16)[:, :, first:last, :],
                in_=plane[:].rearrange("p (c i t) -> p c t i", t=PACK, i=16)[:, :, first:last, :],
            )

        w1sd = held.tile([P, H], U8, name="w1sd", align_bytes=64)
        xg = held.tile([P, S], U32, name="xg", align_bytes=64)
        xgs = held.tile([P, S], U8, name="xgs", align_bytes=64)

        def half(h):
            return slice(h * HALF, (h + 1) * HALF), slice(h * HALF // 16, (h + 1) * HALF // 16)

        win = [held.tile([P, S], F32, name="win%d" % t, align_bytes=64) for t in range(PACK)]
        own = [[held.tile([P, HALF], F32, name="own%d_%d" % (h, t), tag="own%d_%d" % (h, t), align_bytes=64) for t in range(PACK)] for h in range(2)]

        def project(t, h):
            cols = half(h)[0]
            bank = psum.tile([P, S], F32, name="bank%d" % (2 * t + h))
            nc.tensor.matmul_mx(
                out=bank[:, 0:HALF],
                lhsT=w1d[:, t * P : (t + 1) * P].bitcast(FP8X4),
                lhsT_scale=w1sd[:, t * P : (t + 1) * P],
                rhs=xg[:, cols].bitcast(FP8X4),
                rhs_scale=xgs[:, cols],
                start=True,
                stop=True,
            )
            if t == 0 and h == 1:
                nc.vector.tensor_copy(out=win[t][:, cols], in_=bank[:, 0:HALF])
            else:
                nc.scalar.copy(out=win[t][:, cols], in_=bank[:, 0:HALF])
            if h == 0 and t < 2:
                nc.scalar.copy(out=own[0][t][:], in_=bank[:, 0:HALF])
            else:
                nc.sync.dma_start(out=own[h][t][:], in_=win[t][:, cols])

        nc.vector.tensor_copy(out=xgs[:], in_=xs[:].indirect(offs_t[:]))
        w1d = deal_words("w1d", w1w)
        for h in range(2):
            cols, ocols = half(h)
            nc.vector.tensor_copy(out=xg[:, cols], in_=xw[:].bitcast(U32).indirect(offs_t[:, ocols]))
            if h == 0:
                deal_bytes(w1sd, w1s, 0, 1)
        deal_bytes(w1sd, w1s, 1, PACK)
        for t in range(PACK):
            for h in range(2):
                project(t, h)
        w2d = deal_words("w2d", w2w)

        zc = held.tile([P, S], U32, name="zc", align_bytes=64)
        zs = held.tile([P, S], U8, name="zs", align_bytes=64)
        oc = held.tile([P, S], I32, name="oc", align_bytes=64)
        osc = held.tile([P, S], U8, name="osc", align_bytes=64)
        out_rows = out_0.rearrange("(p t) j -> p t j", t=PACK)
        out_words = words_view(out_1)
        def rows(name, tag):
            return held.tile([P, PACK, HALF], F32, name=name, tag=tag, align_bytes=64)

        diff = {(n, h): rows("diff%s%d" % (n, h), "diff%s%d" % (n, h)) for n in "pn" for h in range(2)}
        dist = {(n, h): rows("dist%s%d" % (n, h), "dist%s%d" % (n, h)) for n in "pn" for h in range(2)}
        sig = [rows("sig%d" % h, "sig%d" % h) for h in range(2)]
        lists = {"p": pos_t, "n": neg_t}

        def fetch(n, h, t):
            nc.vector.tensor_tensor(diff[n, h][:, t, :], win[t][:].indirect(lists[n][:, half(h)[1]]), own[h][t][:], ALU.subtract)

        def measure(n, h, first, last):
            nc.scalar.activation(dist[n, h][:, first:last, :], diff[n, h][:, first:last, :], ACT.Abs)
            if n == "p":
                nc.scalar.activation(diff[n, h][:, first:last, :], dist[n, h][:, first:last, :], ACT.Sigmoid)
                for t in range(first, last):
                    nc.scalar.activation(sig[h][:, t, :], diff[n, h][:, t, :], ACT.Copy, scale=gain[:, t : t + 1])

        state = {}

        def part(c):
            return c // 2, slice(c % 2 * CHUNK, (c % 2 + 1) * CHUNK)

        def margin(c):
            h, cols = part(c)
            x = ring.tile([P, PACK, CHUNK], F32, name="x", align_bytes=64, bufs=4)
            nc.vector.scalar_tensor_tensor(x[:], dist["p", h][:, :, cols], 0.5, dist["n", h][:, :, cols], ALU.add, ALU.subtract)
            state["x", c] = x

        def woven(tile):
            return tile[:].rearrange("p (c i) t -> p c t i", i=4)

        def by_tile(tile):
            return tile[:].rearrange("p t (c i) -> p c t i", i=4)

        def gated(c):
            h, cols = part(c)
            zn = ring.tile([P, PACK, CHUNK], BF16, name="zn", align_bytes=64, bufs=4)
            nc.vector.scalar_tensor_tensor(zn[:], state["x", c][:], 0.0, sig[h][:, :, cols], ALU.max, ALU.mult)
            state["zn", c] = zn

        def weave(c):
            z = ring.tile([P, CHUNK, PACK], BF16, name="z", align_bytes=64, bufs=4)
            if c < LATE:
                nc.scalar.copy(out=woven(z), in_=by_tile(state["zn", c]))
            else:
                nc.vector.tensor_copy(out=woven(z), in_=by_tile(state["zn", c]))
            state["z", c] = z

        def second(c):
            cols = slice(c * CHUNK, (c + 1) * CHUNK)
            nc.vector.quantize_mx(out=zc[:, cols].bitcast(FP8X4), scales=zs[:, cols], in_=state["z", c][:].rearrange("p j t -> p (j t)"))
            ob = ring.tile([P, CHUNK, PACK], BF16, name="ob", align_bytes=64, bufs=4)
            of = ring.tile([P, PACK, CHUNK], F32, name="of", align_bytes=64, bufs=4)
            last = c + 1 == chunks
            for first, end in ((0, 2), (2, 4)) if last else ((0, 4),):
                bank = psum.tile([P, S], F32, name="bank%d" % (c + first // 2))
                for t in range(first, end):
                    nc.tensor.matmul_mx(
                        out=bank[:, t * CHUNK : (t + 1) * CHUNK],
                        lhsT=w2d[:, t * P : (t + 1) * P].bitcast(FP8X4),
                        lhsT_scale=w2sd[:, t * P : (t + 1) * P],
                        rhs=zc[:, cols].bitcast(FP8X4),
                        rhs_scale=zs[:, cols],
                        start=True,
                        stop=True,
                    )
                if c < LATE:
                    nc.scalar.copy(out=ob[:], in_=bank[:].rearrange("p (t j) -> p j t", t=PACK))
                sums = bank[:].rearrange("p (t j) -> p t j", t=PACK)[:, first:end, :]
                if c == LATE:
                    nc.vector.tensor_copy(out=of[:, first:end, :], in_=sums)
                else:
                    nc.scalar.copy(out=of[:, first:end, :], in_=sums)
            nc.sync.dma_start(out=out_rows[:, :, cols], in_=of[:])
            state["ob", c] = ob
            state["of", c] = of

        def weave_out(c):
            nc.vector.tensor_copy(out=woven(state["ob", c]), in_=by_tile(state["of", c]))

        def hand_on(c):
            cols = slice(c * CHUNK, (c + 1) * CHUNK)
            nc.vector.quantize_mx(out=oc[:, cols].bitcast(FP8X4), scales=osc[:, cols], in_=state["ob", c][:].rearrange("p j t -> p (j t)"))
            if c % 2:
                nc.sync.dma_start(out=out_words[:, half(c // 2)[0]], in_=oc[:, half(c // 2)[0]])

        for first in (0, 2):
            for h in range(2):
                for t in (first, first + 1):
                    fetch("p", h, t)
                    fetch("n", h, t)
                    if t == 0 and h == 0:
                        w2sd = held.tile([P, N], U8, name="w2sd", tag="own0_0", align_bytes=64)
                        deal_bytes(w2sd, w2s, 0, PACK)
                    measure("p", h, t, t + 1)
                    measure("n", h, t, t + 1)
        margin(0)
        margin(1)
        gated(0)
        weave(0)
        gated(1)
        weave(1)
        margin(2)
        second(0)
        gated(2)
        margin(3)
        second(1)
        weave(2)
        gated(3)
        second(2)
        weave(3)
        second(3)
        hand_on(0)
        hand_on(1)
        weave_out(2)
        weave_out(3)
        hand_on(2)
        hand_on(3)
        for q in range(4):
            queue = nc.scalar if q % 2 else nc.sync
            queue.dma_start(out=out_2[0, 4 * q : 4 * q + 4, :].bitcast(I32), in_=osc[32 * q : 32 * q + 4, :].bitcast(I32))
